import numpy as np, ml_dtypes
CORES = [83,85,87,115,117,119]
N = 6
BF = ml_dtypes.bfloat16
W, L, B, CAP, C, S, RO = 4096, 256, 16, 128, 7, 32, 6
def work(rng, *shape):
    return B * rng.integers(0, L, shape) + rng.integers(0, RO, shape)
def land(rng, *shape):
    return S * rng.integers(0, CAP, shape) + RO + rng.integers(0, RO, shape)
def parts(rng):
    X = rng.integers(0, 256, (N, 8, 16, W)); R = rng.integers(0, W, (N, 8, 16, W)); R = np.where(rng.random(R.shape) < 0.5, R[:, :, :1], R)
    z = rng.random((N, 8, W)); A = np.where(z < 0.3, work(rng, N, 8, W), np.where(z < 0.5, land(rng, N, 8, W), rng.integers(0, W, (N, 8, W))))
    return X, R, A, rng.integers(0, 256, (N, 8, 16)), rng.integers(1000, 1250, (N, 8, 1)) + rng.integers(0, 200, (N, 8, 16))
def pack(X, R, A, w, th):
    return {"xc": np.ascontiguousarray(X.reshape(N, 128, W)).astype(np.float32).astype(BF), "rf": np.ascontiguousarray(R.reshape(N, 128, W)).astype(np.int32),
            "an": np.ascontiguousarray(A).astype(np.int32), "w": w.reshape(N, 128, 1).astype(np.int32), "th": th.reshape(N, 128, 1).astype(np.int32)}
def setup_inputs(rng):
    return pack(*parts(rng))
def setup_inputs_copies(rng):
    X, R, A, w, th = parts(rng); x = np.arange(W)
    R[:, 1::4] = np.repeat(R[:, 1::4, :1], 16, axis=2)
    R[:, 2::4, 1:] = (R[:, 2::4, :1] + rng.integers(1, W, (N, 2, 15, W))) & (W - 1)
    A[:, ::2] = (x - B) & (W - 1)
    A[:, 1::2] = np.where(rng.random((N, 4, W)) < 0.5, land(rng, N, 4, W), work(rng, N, 4, W))
    th = rng.choice(np.array([1100, 1300, 1500]), (N, 8, 1)) + rng.integers(0, 200, (N, 8, 16))
    return pack(X, R, A, w, th)
def setup_inputs_corners(rng):
    X, R, A, w, th = parts(rng); kk = np.arange(16).reshape(1, 1, 16, 1); x = np.arange(W); heads = B * np.arange(L); off = x & (B - 1)
    X = rng.integers(0, 4, (N, 8, 16, W)); R = rng.integers(0, W, (N, 8, 16, W))
    first = R[:, :, :1]; first = np.where((first & (B - 1)) == 0, first ^ 1, first)
    R = np.where((rng.random(R.shape) < 0.5) | (kk == 0), first, R)
    R = np.where(((R + 613 * kk) & (B - 1)) == 0, R ^ 1, R)
    th = rng.integers(49, 101, (N, 8, 16)); slow = []
    for q in range(N):
        for g in range(8):
            k = int(rng.choice(np.array([0, 1, CAP - 1, CAP, CAP + 1, L])))
            if q == 0: k = (CAP, CAP + 1, L, CAP - 1, 1, 0, CAP, CAP + 1)[g]
            if q == 1: k = (CAP, CAP - 1, 1, 0, 0, 0, 0, 256 - 2 * CAP)[g]
            if q == 2: k = 31 + int(g < 7)
            if q == N - 1 and g == 7: k = CAP
            o = rng.permutation(L)
            if g == 7 and k > 0:
                i = int(np.flatnonzero(o < k)[-1]); o[[i, L - 1]] = o[[L - 1, i]]
            go = o < k; h = np.where(go, 0, rng.integers(100, 256, (16, L))); near = rng.integers(10, 13, (16, L))
            if q == 1: h = np.where(~go & (rng.random(L) < 0.5), near, h)
            if q == 2:
                h = np.where(o < 56, 0, np.where(o < 186, near, h)); slow.append(heads[(o >= k) & (o < 186)])
            X[q, g][:, heads] = h
    w[:, 0::4] = 255; w[:, 1::4] = 0; w[1:3] = 0
    A[:, 0] = x; A[:, 1] = (W - 1) * rng.integers(0, 2, (N, W)); A[:, 2] = (x + 1) & (W - 1); A[:, 3] = (x - B) & (W - 1); A[:, 5] = (x - 1) & (W - 1)
    A[:, 6] = np.where(rng.random((N, W)) < 0.5, x, W - 1 - x)
    X[2][:, :, off == 1] = rng.integers(100, 256, (8, 16, L))
    to = B * rng.integers(0, L, (8, 16, W)) + np.where(off == 2, 1, rng.integers(2, B, (8, 16, W)))
    R[2] = (to - 613 * kk[0]) & (W - 1)
    A[2] = B * rng.integers(0, L, (8, W)) + 3
    A[2][:, 2 * B * np.arange(L // 2) + 2] = 2 * B * rng.integers(0, L // 2, (8, L // 2)) + B + 2
    for g in range(8): A[2, g, slow[g]] = 2 * B * rng.integers(0, L // 2, len(slow[g])) + 2
    return pack(X, R, A, w, th)
def setup_inputs_ends(rng):
    kind = rng.integers(0, 3, (N, 8, 1, W)); X = 255 * np.where(kind == 2, rng.integers(0, 2, (N, 8, 16, W)), kind)
    R = (W - 1) * rng.integers(0, 2, (N, 8, 16, W)); A = (W - 1) * rng.integers(0, 2, (N, 8, W))
    z = rng.random((N, 8, W)); A = np.where(z < 0.12, work(rng, N, 8, W), np.where(z < 0.25, land(rng, N, 8, W), A))
    w = 255 * rng.integers(0, 2, (N, 8, 16)); th = np.zeros((N, 8, 16), np.int64)
    for q in range(N):
        many = np.append(rng.permutation(np.array([C, C - 1, C - 2, C + 1, C - 1, C, C - 1])), C)
        i = int(np.flatnonzero(many == C)[0]); many[[i, 6]] = many[[6, i]]
        for g in range(8): th[q, g, rng.permutation(16)[:many[g]]] = 4080
    w[:, 7] = 255; w[:, 6] = 0; w[:, 6, 0] = 255; w[:, 6, 1] = 1
    for x in (0, W - B):
        X[:, 7, :, x] = 255; A[:, 7, x] = 0
    X[:, 6, 0, W - B] = 16; X[:, 6, 1, W - B] = 15; A[:, 6, W - B] = W - 1; R[:, 6, 0, W - B] = 0
    X[:, 6, 0, 0] = 15; X[:, 6, 1, 0] = 250; A[:, 6, 0] = W - 2; R[:, 6, 0, 0] = 0
    R[:, 6, :, W - 1] = W - 1
    R[:, 6, :, W - 2] = W - 3
    R[:, 7, 0, 0] = W - 1; R[:, 7, 14:, 0] = 0
    X[:, 7, :, (613 * 15) & (W - 1)] = 0; X[:, 7, :, (613 * 14) & (W - 1)] = 255
    return pack(X, R, A, w, th)
def setup_inputs_spread(rng):
    X = (rng.random((N, 8, 16, W)) * np.exp2(rng.integers(0, 9, (N, 8, 1, W)))).astype(np.int64)
    p = rng.choice(np.array([1, 2, 4]), (N, 8, 16, 1)); R = np.minimum((W * rng.random((N, 8, 16, W)) ** p).astype(np.int64), W - 1)
    R = np.where(rng.random(R.shape) < rng.random((N, 8, 1, W)), R[:, :, :1], R)
    p = rng.choice(np.array([1, 2, 4]), (N, 8, 1)); A = np.minimum((W * rng.random((N, 8, W)) ** p).astype(np.int64), W - 1)
    w = np.minimum(np.exp2(8 * rng.random((N, 8, 16))).astype(np.int64), 255) * (rng.random((N, 8, 16)) > 0.1)
    p = rng.choice(np.array([1, 2, 4, 8]), (N, 8, 1)); th = np.minimum((4081 * rng.random((N, 8, 16)) ** p).astype(np.int64), 4080)
    return pack(X, R, A, w, th)
def setup_inputs_ties(rng):
    X, R, A, w, th = parts(rng)
    pool = rng.integers(0, 256, (N, 8, 16, 6)); X = np.take_along_axis(pool, rng.integers(0, 6, (N, 8, 1, W)), 3)
    i = rng.integers(0, 6, (N, 8, 1, 16)); j = rng.integers(0, 6, (N, 8, 1, 16))
    d = np.add.reduce(np.abs(np.take_along_axis(pool, i, 3) - np.take_along_axis(pool, j, 3)), axis=2)
    return pack(X, R, A, w, np.minimum(d + rng.integers(0, 2, d.shape), 4080))
def check_inputs(d):
    bad = []
    for k, lo, hi in (("xc", 0, 255), ("rf", 0, W - 1), ("an", 0, W - 1), ("w", 0, 255), ("th", 0, 4080)):
        a = np.asarray(d[k]).astype(np.float64)
        if not (np.min(a) >= lo and np.max(a) <= hi): bad.append("range of " + k)
        elif np.any(a != np.floor(a)): bad.append("whole numbers in " + k)
    return bad
def cols(T, ix):
    return np.take_along_axis(T, ix[:, :, None, :], 3)
def dist(X, q, u, m):
    kk = np.arange(16).reshape(1, 1, 16, 1); s = ((m * u >> 5) + m + 613 * kk) & (W - 1)
    x = cols(X, s.reshape(N, 8, 16 * L)).reshape(N, 8, 16, 16, L)
    return np.add.reduce(np.abs(x - q[:, :, :, None, :]), axis=2).astype(np.int64)
def reference(xc, rf, an, w, th):
    X = xc.astype(np.float32).astype(np.int32).reshape(N, 8, 16, W); R = rf.astype(np.int64).reshape(N, 8, 16, W); A = an.astype(np.int64)
    ww = w.astype(np.int64).reshape(N, 8, 16, 1); tt = th.astype(np.int64).reshape(N, 8, 16, 1)
    v = np.zeros((N, 8, 1), np.int64) + B * np.arange(L); a = np.take_along_axis(A, v, 2); b = np.zeros((N, 1, 1, 1), np.int64)
    for t in range(RO):
        q = cols(X, v); u = np.add.reduce(ww * q, axis=2, keepdims=True) & 4095
        e = cols(R, a); own = np.take_along_axis(R[:, :, 0], v, 2)[:, :, None, :]
        n = np.where(e == e[:, :, :1], own, e)
        d, d2 = dist(X, q, u, e), dist(X, q, u, n)
        f = np.where(d2 < d, n, e); f[:, :, 0] = own[:, :, 0]
        fit = (np.add.reduce((np.minimum(d, d2) < tt + b).astype(np.int64), axis=2) >= C).astype(np.int64)
        b = (np.add.reduce(fit, axis=(1, 2)) & 255).reshape(N, 1, 1, 1)
        after = np.where(fit == 1, np.take_along_axis(A, v + 1, 2), np.take_along_axis(A, a, 2))
        r, g, i = np.nonzero(fit)
        R[r, g, :, v[r, g, i]] = f[r, g, :, i]; A[r, g, v[r, g, i]] = a[r, g, i]
        before = np.add.accumulate(fit, axis=2) - fit
        r, g, i = np.nonzero((fit == 1) & (before < CAP))
        R[(r + 1 + t % (N - 1)) % N, g, :, S * before[r, g, i] + RO + t] = f[r, g, :, i]
        v = v + fit; a = after
    o = R.reshape(N, 8, 16, L, B); o = o[..., :RO // 2] + 4096 * o[..., RO // 2:RO]
    h = R.reshape(N, 8, 16, CAP, S)[..., RO:2 * RO]
    return {"yr": o.reshape(N, 128, L * (RO // 2)).astype(np.float32), "yh": h.reshape(N, 128, CAP * RO).astype(np.float32),
            "yan": A.reshape(N, 8, L, B)[..., :RO].reshape(N, 8, L * RO).astype(np.float32), "yv": v.astype(np.float32), "ya": a.astype(np.float32)}

@@ -1,0 +1,473 @@
+import math
+from concourse.mybir import AluOpType as OP, ActivationFunctionType as AF
+
+
+def _scratch():
+    f, b, i, u = "float32", "bfloat16", "int32", "uint16"
+    s = {}
+    def sb(dtype, **kw):
+        for n, w in kw.items():
+            s[n] = ("sbuf", [128, w], dtype)
+    sb(b, X=12288, Q=1536, qrep=4096, WK=2048, SB=2048, BM=128, rmp=128, rmBM=128, krBM=128, Ibf=128, nI=128, Gt=128,
+       U2=128, ones=128, Wu=128, Ahi=256, Alo=256, df0=1024, df1=1024, df2=1024, ab0=1024, ab1=1024, Xg0=1024, Xg1=1024,
+       Ea0=1024, Ea1=1024, sf=256, fT=16, incl=16)
+    sb(i, Ri=4096, Ab=256, Ai1=256, Ai2=256, wi=1, thi=1, pi=1, ri=256, colsi=16, rgi=128, rmi=256, ui=512,
+       uj=512, t1=256, t2=256, l1=256, l2=256)
+    sb(f, R=8192, A=8192, U=1536, O=1536, E=1536, VT=1792, colsf=16, B0f=128, IBf=128, I1f=128, diag=256, rz=256,
+       dup=32, dupT=32, e=256, u=256, t3=256, l3=256, penal=256, Ep=256, Es=256, oe=256, mn=256, sub=256, prod=256,
+       tile=320, am=256, sc=256, arep0=256, arep1=256, land=768, stage=768, yht=768)
+    sb(b, q=256)
+    sb(u, pl=256, aL=16, vcL=16, selL=16, offm=16, offR=16)
+    for k in range(6):
+        s["msg%d" % k] = ("sbuf", [128, 512], f)
+        s["PLE%d" % k] = ("sbuf", [128, 256], u)
+    for k in range(8):
+        s["p%d" % k] = ("psum", [128, 512], f)
+    return s
+
+
+SCRATCH = _scratch()
+SEMAPHORES = (["cv", "cs", "ct", "cg", "ls", "out"] + ["ld%d" % k for k in range(9)]
+              + ["pre%d" % k for k in range(6)] + ["arr%d" % k for k in range(6)])
+STEPS, LANES, COLS, CHUNK = 6, 256, 4096, 64
+VREP = 12
+
+
+def rank_program(g, core, T, topo):
+    rank = T.rank_of(core)
+    if rank is None:
+        return
+    cores, n = T.cores, len(T.cores)
+    eng = {"v": g.vector, "s": g.scalar, "t": g.tensor, "g": g, "y": g.sync}
+    qsem = {"v": "cv", "s": "cs", "t": "ct", "g": "cg"}
+    count = {"cv": 0, "cs": 0, "ct": 0, "cg": 0}
+    known = {q: {} for q in eng}
+    clock = {}
+    hist = {}
+
+    small = {}
+    for k, x in enumerate("pgi pmi odi cki bi bj".split()):
+        small[x] = ("colsi", k, k + 1)
+    for k, x in enumerate("pgf pmf odf evf pm1 ckf k0n wf thf thb".split()):
+        small[x] = ("colsf", k, k + 1)
+    for k, x in enumerate("iT D0m tA tB y nf f256 dd y1 y2 y3 aT vT0 vT1 vc0 vc1".split()):
+        small[x] = ("tile", 16 * k, 16 * k + 16)
+    alias = {"yrt": "U", "yant": "E", "vrep": "l3"}
+
+    def r(name, a=0, b=None, step=1):
+        if name in small:
+            return small[name] + (1,)
+        name = alias.get(name, name)
+        return (name, a, SCRATCH[name][1][1] if b is None else b, step)
+
+    def ap(x):
+        if not isinstance(x, tuple):
+            return x
+        if x[0] == "ind":
+            return ap(x[1]).indirect(ap(x[2]))
+        return T[x[0]][:, x[1]:x[2]] if x[3] == 1 else T[x[0]][:, x[1]:x[2]:x[3]]
+
+    def parts(x):
+        if not isinstance(x, tuple):
+            return []
+        return [x[1], x[2]] if x[0] == "ind" else [x]
+
+    def meet(x, y):
+        return x[1] < y[2] and y[1] < x[2] and (x[1] - y[1]) % math.gcd(x[3], y[3]) == 0
+
+    def covers(x, y):
+        return x[1:] == y[1:] or (x[3] == 1 and x[1] <= y[1] and x[2] >= y[2])
+
+    def wait(q, sem, val):
+        if known[q].get(sem, 0) >= val:
+            return
+        eng[q].wait_ge(T.sem[sem], val)
+        for s, v in list(clock.get((sem, val), {}).items()) + [(sem, val)]:
+            known[q][s] = max(known[q].get(s, 0), v)
+
+    def order(q, reads, writes, inner=False):
+        need = {}
+        for regs, w in ((reads, False), (writes, True)):
+            for x in regs:
+                psum = SCRATCH[x[0]][0] == "psum"
+                for y, yw, yq, sem, val in hist.get(x[0], []):
+                    if psum and yq != q:
+                        hit = True
+                    else:
+                        hit = (w or yw) and meet(x, y) and not (inner and yq == q)
+                    if hit:
+                        need[sem] = max(need.get(sem, 0), val)
+        for sem in sorted(need):
+            wait(q, sem, need[sem])
+
+    def note(q, reads, writes, sem, val):
+        for regs, w in ((reads, False), (writes, True)):
+            for x in regs:
+                h = hist.setdefault(x[0], [])
+                if w:
+                    h[:] = [z for z in h if not covers(x, z[0])]
+                else:
+                    h[:] = [z for z in h if z[1] or z[2] != q or not covers(x, z[0])]
+                h.append((x, w, q, sem, val))
+
+    def emit(q, call, reads, writes, inner=False):
+        order(q, reads, writes, inner)
+        sem = qsem[q]
+        count[sem] += 1
+        call().then_inc(T.sem[sem], 1)
+        clock[(sem, count[sem])] = dict(known[q])
+        note(q, reads, writes, sem, count[sem])
+
+    def many(*xs):
+        return [y for x in xs for y in parts(x)]
+
+    def outs(x):
+        return ([x[1]], [x[2]]) if x[0] == "ind" else ([x], [])
+
+    def tt(out, in0, in1, op):
+        w, o = outs(out)
+        emit("v", lambda: g.vector.tensor_tensor(ap(out), ap(in0), ap(in1), op), many(in0, in1) + o, w)
+
+    def ts(out, in0, s1, s2, op0, op1=None):
+        if op1 is None:
+            emit("v", lambda: g.vector.tensor_scalar(ap(out), ap(in0), ap(s1), None, op0), many(in0, s1), [out])
+        else:
+            emit("v", lambda: g.vector.tensor_scalar(ap(out), ap(in0), ap(s1), ap(s2), op0, op1), many(in0, s1, s2), [out])
+
+    def tc(out, in_):
+        w, o = outs(out)
+        emit("v", lambda: g.vector.tensor_copy(ap(out), ap(in_)), many(in_) + o, w)
+
+    def fill(out, value):
+        emit("v", lambda: g.vector.memset(ap(out), value), [], [out])
+
+    def scan(out, d0, d1, op0, op1):
+        emit("v", lambda: g.vector.tensor_tensor_scan(ap(out), ap(d0), ap(d1), 0.0, op0, op1), many(d0, d1), [out])
+
+    def act(out, in_, func=AF.Copy, scale=None, bias=None):
+        kw = {}
+        if scale is not None:
+            kw["scale"] = ap(scale)
+        if bias is not None:
+            kw["bias"] = ap(bias)
+        emit("s", lambda: g.scalar.activation(ap(out), ap(in_), func, **kw), many(in_, scale, bias), [out])
+
+    def mm(out, lhsT, rhs, start=True, stop=True):
+        emit("t", lambda: g.tensor.matmul(ap(out), ap(lhsT), ap(rhs), start, stop), many(lhsT, rhs), [out], inner=not start)
+
+    def iota(out, pattern, base, cm, flag=False):
+        if flag:
+            emit("g", lambda: g.iota(ap(out), pattern, base, cm, allow_small_or_imprecise_dtypes=True), [], [out])
+        else:
+            emit("g", lambda: g.iota(ap(out), pattern, base, cm), [], [out])
+
+    def load(sem, out, src):
+        g.sync.dma_start(ap(out), src).then_inc(T.sem[sem], 16)
+        note("y", [], [out], sem, 16)
+
+    def store(out, src, x):
+        order("y", [x], [])
+        g.sync.dma_start(out, src).then_inc(T.sem["out"], 16)
+        stores[0] += 16
+
+    stores = [0]
+    sent = [0]
+
+    def send(dst, out, in_, sem):
+        order("g", [in_], [])
+        rid, pid, _ = topo.addr(dst)
+        g.remote_dma(ap(out), ap(in_), T.sem[sem], T.sem["ls"], pid, rid, topo.mask(core, dst))
+        sent[0] += len(topo.engines(core, dst))
+
+    def will_land(x, sem, src):
+        note("x", [], [x], sem, len(topo.engines(src, core)))
+
+    def to(t):
+        return cores[(rank + 1 + t % (n - 1)) % n]
+
+    def frm(t):
+        return cores[(rank - 1 - t % (n - 1)) % n]
+
+    load("ld0", r("Ab"), T.an[:])
+    load("ld1", r("wi"), T.w[:])
+    load("ld2", r("thi"), T.th[:])
+    load("ld3", r("X", 0, COLS), T.xc[:])
+    for k in range(4):
+        load("ld%d" % (4 + k), r("Ri", 1024 * k, 1024 * k + 1024), T.rf[:, 1024 * k:1024 * k + 1024])
+    for t in range(STEPS):
+        will_land(r("msg%d" % t, 0, 128), "pre%d" % t, to(t))
+        will_land(r("land", 128 * t, 128 * t + 128), "arr%d" % t, frm(t))
+
+    iota(r("pi"), [[0, 1]], 0, 1)
+    iota(r("ri"), [[1, 256]], 0, 0)
+    iota(r("VT"), [[1, 7], [16, 256]], 0, 0, True)
+    fill(r("ones"), 1.0)
+    ts(r("pgi"), r("pi"), 4, None, OP.arith_shift_right)
+    ts(r("pmi"), r("pi"), 15, None, OP.bitwise_and)
+    ts(r("rgi"), r("ri", 0, 128), 4, None, OP.arith_shift_right)
+    ts(r("rmi"), r("ri"), 15, None, OP.bitwise_and)
+    ts(r("odi"), r("pgi"), 1, None, OP.bitwise_and)
+    tc(r("pgf"), r("pgi"))
+    tc(r("pmf"), r("pmi"))
+    tc(r("odf"), r("odi"))
+    ts(r("BM"), r("rgi"), r("pgf"), None, OP.is_equal)
+    ts(r("rmp"), r("rmi", 0, 128), 1.0, None, OP.add)
+    ts(r("pm1"), r("pmf"), 1.0, None, OP.add)
+    ts(r("evf"), r("odf"), -1.0, 1.0, OP.mult, OP.add)
+    tt(r("rmBM"), r("rmp"), r("BM"), OP.mult)
+    ts(r("krBM"), r("BM"), r("pm1"), None, OP.mult)
+    ts(r("Ai1"), r("Ab"), 4032, None, OP.bitwise_and)
+    ts(r("Ai2"), r("Ab"), 63, None, OP.bitwise_and)
+    tc(r("Ahi"), r("Ai1"))
+    tc(r("Alo"), r("Ai2"))
+    for k in range(16):
+        ts(r("SB", 128 * k, 128 * k + 128), r("krBM"), float(k + 1), None, OP.is_equal)
+    for k in range(16):
+        bank = ("p0", "p1", "p3", "p4")[k // 2 % 4]
+        x = r(bank, 256 * (k % 2), 256 * (k % 2) + 256)
+        mm(x, r("SB", 128 * k, 128 * k + 128), r("Ahi"), True, False)
+        mm(x, r("SB", 128 * k, 128 * k + 128), r("Alo"), False, True)
+        if k % 2:
+            act(r("A", 256 * k - 256, 256 * k + 256), r(bank))
+    for k in range(16):
+        ts(r("WK", 128 * k, 128 * k + 128), r("rmBM"), float(k + 1), None, OP.is_equal)
+    tc(r("dup", 0, 16), r("Ab", 0, 256, 16))
+    tc(r("dup", 16, 32), r("Ab", 0, 256, 16))
+    ts(r("Ibf"), r("rmBM"), r("pm1"), None, OP.is_equal)
+    emit("v", lambda: g.vector.transpose(ap(r("dupT")), ap(r("dup"))), [r("dup")], [r("dupT")])
+    ts(r("Gt"), r("rmBM"), r("pm1"), None, OP.is_le)
+    ts(r("I1f"), r("Ibf"), -1023.0, None, OP.mult)
+    ts(r("tA"), r("dupT", 0, 16), r("evf"), None, OP.mult)
+    ts(r("tB"), r("dupT", 16, 32), r("odf"), None, OP.mult)
+    tt(r("Gt"), r("Gt"), r("BM"), OP.mult)
+    tt(r("aT"), r("tA"), r("tB"), OP.add)
+    tt(r("U2"), r("I1f"), r("Gt"), OP.subtract)
+    tc(r("aL"), r("aT"))
+    ts(r("nI"), r("Ibf"), -1.0, None, OP.mult)
+    tc(r("B0f"), r("SB", 0, 128))
+    tt(r("IBf"), r("Ibf"), r("SB", 0, 128), OP.subtract)
+    ts(r("diag"), r("rmi"), r("pmf"), None, OP.is_equal)
+    ts(r("rz"), r("rmi"), 0.5, None, OP.is_gt)
+    ts(r("iT"), r("ri", 0, 16), 16.0, r("pmf"), OP.mult, OP.add)
+    ts(r("cki"), r("pmf"), 613.0, None, OP.mult)
+    ts(r("k0n"), r("pmf"), 0.5, -1000000.0, OP.is_lt, OP.mult)
+    ts(r("vT0"), r("iT"), 16.0, None, OP.mult)
+    ts(r("cki"), r("cki"), 4095, None, OP.bitwise_and)
+    tc(r("vc0"), r("iT"))
+    ts(r("D0m"), r("iT"), -767.0, None, OP.add)
+    tc(r("ckf"), r("cki"))
+    tc(r("wf"), r("wi"))
+    tc(r("thf"), r("thi"))
+    ts(r("Wu"), r("BM"), r("wf"), None, OP.mult)
+    tc(r("thb"), r("thi"))
+    act(r("arep0"), r("A", 0, COLS, 16))
+
+    for s in range(STEPS):
+        tc(r("Q", 256 * s, 256 * s + 256), r("X", s, COLS, 16))
+    act(r("X", 8192, 12288), r("X", 0, COLS))
+    for h in range(3):
+        bank = ("p2", "p5", "p6")[h]
+        mm(r(bank), r("Wu"), r("Q", 512 * h, 512 * h + 512))
+    for h in range(3):
+        bank = ("p2", "p5", "p6")[h]
+        tc(r("ui"), r(bank))
+        ts(r("uj"), r("ui"), 4095, None, OP.bitwise_and)
+        tc(r("U", 512 * h, 512 * h + 512), r("uj"))
+        if h == 0:
+            for k in range(16):
+                tc(r("qrep", k, 4096, 16), r("Q", 0, 256))
+    tc(r("X", 4096, 8192), r("X", 0, COLS))
+    for k in range(4):
+        tc(r("R", 1024 * k, 1024 * k + 1024), r("Ri", 1024 * k, 1024 * k + 1024))
+
+    def own(s):
+        mm(r("p7", 0, 256), r("B0f"), r("R", s, COLS, 16))
+
+    def own_list(s):
+        x = r("p7", 0, 256)
+        tt(r("l1"), x, r("U", 256 * s, 256 * s + 256), OP.mult)
+        ts(r("l2"), r("l1"), 5, 4095, OP.arith_shift_right, OP.bitwise_and)
+        tt(r("l3"), r("l2"), x, OP.add)
+        ts(r("PLE%d" % s), r("l3"), r("ckf"), None, OP.add)
+        act(r("O", 256 * s, 256 * s + 256), x)
+
+    def e_gather(s, p):
+        act(r("Xg%d" % (p % 2)), ("ind", r("X"), r("PLE%d" % s, 64 * p, 64 * p + 64)))
+
+    def e_minus(s, p):
+        for k in range(16):
+            x = r("p%d" % (k // 8), 64 * (k % 8), 64 * (k % 8) + 64)
+            mm(x, r("Ibf"), r("Xg%d" % (p % 2), k, 1024, 16), True, False)
+            mm(x, r("nI"), r("Q", 256 * s + 64 * p, 256 * s + 64 * p + 64), False, True)
+
+    def e_abs(p):
+        for h in range(2):
+            act(r("Ea%d" % (p % 2), 512 * h, 512 * h + 512), r("p%d" % h), AF.Abs)
+
+    def e_sum(p):
+        for k in range(16):
+            mm(r("p2", 64 * p, 64 * p + 64), r("WK", 128 * k, 128 * k + 128),
+               r("Ea%d" % (p % 2), 64 * k, 64 * k + 64), k == 0, k == 15)
+
+    def e_store(s):
+        act(r("E", 256 * s, 256 * s + 256), r("p2", 0, 256))
+
+    def d_gather(lst, c, b):
+        tt(r("df%d" % b), ("ind", r("X"), r(lst, 64 * c, 64 * c + 64)), r("qrep", 1024 * c, 1024 * c + 1024), OP.subtract)
+
+    def d_abs(b, b2):
+        act(r("ab%d" % b2), r("df%d" % b), AF.Abs)
+
+    def d_sum(bank, c, b2):
+        for k in range(16):
+            mm(r(bank, 64 * c, 64 * c + 64), r("WK", 128 * k, 128 * k + 128), r("ab%d" % b2, k, 1024, 16), k == 0, k == 15)
+
+    nbuf = [0, 0]
+
+    def d_chunk(lst, bank, c):
+        b, b2 = nbuf[0] % 3, nbuf[0] % 2
+        nbuf[0] += 1
+        d_gather(lst, c, b)
+        d_abs(b, b2)
+        d_sum(bank, c, b2)
+
+    own(0)
+    for t in range(STEPS):
+        last = t == STEPS - 1
+        va, vb = "vT%d" % (t % 2), "vT%d" % ((t + 1) % 2)
+        ca, cb = "vc%d" % (t % 2), "vc%d" % ((t + 1) % 2)
+        ra, rb = "arep%d" % (t % 2), "arep%d" % ((t + 1) % 2)
+        rw = r("R", 0, COLS)
+        if t > 0:
+            tc(r("R", 6 + t - 1, COLS, 32), r("land", 128 * t - 128, 128 * t))
+        act(r("e"), ("ind", rw, r("aL")))
+        u = r("u") if t else r("U", 0, 256)
+        tt(r("t1"), ("ind", rw, r("aL")), u, OP.mult)
+        ts(r("t2"), r("t1"), 5, 4095, OP.arith_shift_right, OP.bitwise_and)
+        tt(r("t3"), r("t2"), r("e"), OP.add)
+        ts(r("pl"), r("t3"), r("ckf"), None, OP.add)
+        mm(r("p5", 0, 256), r("IBf"), r("e"))
+        act(r("penal"), r("p5", 0, 256), AF.Abs, scale=8192.0)
+        if t == 0:
+            own_list(0)
+            own(1)
+            e_gather(0, 0)
+            d_chunk("pl", "p3", 0)
+            e_minus(0, 0)
+            d_chunk("PLE0", "p2", 1)
+            e_abs(0)
+            e_sum(0)
+            d_chunk("pl", "p3", 1)
+            d_chunk("PLE0", "p2", 2)
+            d_chunk("pl", "p3", 2)
+            d_chunk("PLE0", "p2", 3)
+            own_list(1)
+            e_store(0)
+            for k in range(STEPS):
+                act(r("stage", 128 * k, 128 * k + 128), r("R", 6 + k, COLS, 32))
+                send(frm(k), r("msg%d" % k, 0, 128), r("stage", 128 * k, 128 * k + 128), "pre%d" % k)
+        else:
+            e_gather(t, 3)
+            d_chunk("pl", "p3", 0)
+            e_abs(2)
+            e_sum(2)
+            e_minus(t, 3)
+            d_chunk("pl", "p3", 1)
+            e_abs(3)
+            e_sum(3)
+            d_chunk("pl", "p3", 2)
+            e_store(t)
+        d_chunk("pl", "p4", 3)
+        if t:
+            tt(r("Ep"), ("ind", r("E", 0, 256 * t + 256), r("vcL")), r("penal"), OP.add)
+            tt(r("oe"), ("ind", r("O", 0, 256 * t + 256), r("vcL")), r("e"), OP.subtract)
+        else:
+            tt(r("Ep"), r("E", 0, 256), r("penal"), OP.add)
+            tt(r("oe"), r("O", 0, 256), r("e"), OP.subtract)
+        act(r("Es"), r("Ep"), AF.Identity, bias=r("k0n"))
+        if t + 2 < STEPS:
+            own(t + 2)
+            own_list(t + 2)
+        if t + 1 < STEPS:
+            e_gather(t + 1, 0)
+            e_gather(t + 1, 1)
+        x0, x1 = (0, 192), (192, 256)
+        for (a, b), bank in ((x0, "p3"), (x1, "p4")):
+            tt(r("mn", a, b), r("Ep", a, b), r(bank, a, b), OP.min)
+            ts(r("sf", a, b), r("mn", a, b), r("thb"), None, OP.is_lt)
+        for k in range(16):
+            mm(r("p6", 0, 16), r("WK", 128 * k, 128 * k + 128), r("sf", k, 256, 16), k == 0, k == 15)
+        for (a, b), bank in ((x0, "p3"), (x1, "p4")):
+            tt(r("sub", a, b), r("Es", a, b), r(bank, a, b), OP.is_lt)
+        tt(r("prod"), r("sub"), r("oe"), OP.mult)
+        ts(r("fT"), r("p6", 0, 16), 6.5, None, OP.is_ge)
+        scan(r("incl"), r("ones", 0, 16), r("fT"), OP.mult, OP.add)
+        mm(r("p5", 0, 16), r("U2"), r("fT"), True, False)
+        mm(r("p5", 0, 16), r("BM"), r("incl"), False, True)
+        ts(r("f256"), r("p6", 0, 16), 6.5, 256.0, OP.is_ge, OP.mult)
+        ts(r("nf"), r("p6", 0, 16), 6.5, 4096.0, OP.is_lt, OP.mult)
+        tt(r("y"), r("p5", 0, 16), r("D0m"), OP.min)
+        ts(r("offm"), r("y"), 1023.0, None, OP.add)
+        tt(("ind", r("msg%d" % t), r("offm")), r("e"), r("prod"), OP.add)
+        send(to(t), r("land", 128 * t, 128 * t + 128), r("msg%d" % t, 0, 128), "arr%d" % t)
+        tt(r(cb), r(ca), r("f256"), OP.add)
+        tt(r(vb), r(va), r("fT"), OP.add)
+        tc(r("vcL"), r(cb))
+        tt(r("dd"), r(vb), r("aT"), OP.subtract)
+        tt(r("y1"), r("dd"), r("fT"), OP.mult)
+        tt(r("y3"), r("nf"), r(va), OP.add)
+        tt(r("y2"), r("y1"), r("aT"), OP.add)
+        tc(r("offR"), r("y3"))
+        tc(r("selL"), r("y2"))
+        aw = r("A", 0, COLS)
+        if t + 1 < STEPS:
+            e_minus(t + 1, 0)
+            e_abs(0)
+            e_sum(0)
+            e_minus(t + 1, 1)
+            act(r("q"), ("ind", r("Q"), r("vcL")))
+            act(r("u"), ("ind", r("U"), r("vcL")))
+            act(r(rb), ("ind", aw, r("selL")))
+            for k in range(VREP, 16):
+                act(r("qrep", k, 4096, 16), r("q"))
+            e_gather(t + 1, 2)
+            e_abs(1)
+            e_sum(1)
+            e_minus(t + 1, 2)
+            tt(r("am"), ("ind", aw, r("selL")), r("diag"), OP.mult)
+            scan(r("sc"), r("rz"), r("am"), OP.mult, OP.add)
+            tc(r("aL"), r("sc", 15, 256, 16))
+            tc(r("aT"), r("sc", 15, 256, 16))
+        else:
+            act(r("vrep"), ("ind", r("VT"), r("vcL")))
+            act(r(rb), ("ind", aw, r("selL")))
+        tt(("ind", r("R"), r("offR")), r("e"), r("prod"), OP.add)
+        if not last:
+            mm(r("p6", 64, 65), r("ones"), r("incl", 15, 16))
+            for k in range(VREP):
+                tc(r("qrep", k, 4096, 16), r("q"))
+            tc(r("bi"), r("p6", 64, 65))
+            ts(r("bj"), r("bi"), 255, None, OP.bitwise_and)
+            tt(r("thb"), r("thf"), r("bj"), OP.add)
+        tc(("ind", r("A"), r("offR")), r(ra))
+        if t > 0:
+            act(r("yht", t - 1, 768, 6), r("land", 128 * t - 128, 128 * t))
+
+    store(T.yv[:], T.l3[0:128:16, :], r("vrep"))
+    store(T.ya[:], T["arep%d" % (STEPS % 2)][0:128:16, :], r("arep%d" % (STEPS % 2)))
+    for s in range(3):
+        act(r("p%d" % s, 0, 256), r("R", 3 + s, COLS, 16), AF.Copy, scale=4096.0)
+        tt(r("yrt", s, 768, 3), r("p%d" % s, 0, 256), r("R", s, COLS, 16), OP.add)
+    store(T.yr[:], T.U[:, 0:768], r("yrt", 0, 768))
+    for s in range(6):
+        if s % 2:
+            act(r("yant", s, 1536, 6), r("A", s, COLS, 16))
+        else:
+            tc(r("yant", s, 1536, 6), r("A", s, COLS, 16))
+    store(T.yan[:], T.E[0:128:16, :], r("yant"))
+    tc(r("yht", STEPS - 1, 768, 6), r("land", 128 * STEPS - 128, 128 * STEPS))
+    store(T.yh[:], T.yht[:], r("yht"))
+    for sem in ("cv", "cs", "ct", "cg"):
+        wait("g", sem, count[sem])
+    g.wait_ge(T.sem["ls"], sent[0])
+    g.wait_ge(T.sem["out"], stores[0])

@@ -30,7 +30,7 @@ SCRATCH = _scratch()
 SEMAPHORES = (["cv", "cs", "ct", "cg", "ls", "out"] + ["ld%d" % k for k in range(9)]
               + ["pre%d" % k for k in range(6)] + ["arr%d" % k for k in range(6)])
 STEPS, LANES, COLS, CHUNK = 6, 256, 4096, 64
-VREP = 12
+VREP = 11
 
 
 def rank_program(g, core, T, topo):
@@ -151,6 +151,10 @@ def rank_program(g, core, T, topo):
         if bias is not None:
             kw["bias"] = ap(bias)
         emit("s", lambda: g.scalar.activation(ap(out), ap(in_), func, **kw), many(in_, scale, bias), [out])
+
+    def gcopy(out, in_):
+        k = len(range(out[1], out[2], out[3]))
+        emit("g", lambda: g.affine_select(ap(out), ap(in_), [[0, k]], OP.is_ge, 0.0, 0, 0), [in_], [out])
 
     def mm(out, lhsT, rhs, start=True, stop=True):
         emit("t", lambda: g.tensor.matmul(ap(out), ap(lhsT), ap(rhs), start, stop), many(lhsT, rhs), [out], inner=not start)
@@ -289,7 +293,7 @@ def rank_program(g, core, T, topo):
         ts(r("l2"), r("l1"), 5, 4095, OP.arith_shift_right, OP.bitwise_and)
         tt(r("l3"), r("l2"), x, OP.add)
         ts(r("PLE%d" % s), r("l3"), r("ckf"), None, OP.add)
-        act(r("O", 256 * s, 256 * s + 256), x)
+        tc(r("O", 256 * s, 256 * s + 256), x)
 
     def e_gather(s, p):
         act(r("Xg%d" % (p % 2)), ("ind", r("X"), r("PLE%d" % s, 64 * p, 64 * p + 64)))
@@ -347,11 +351,13 @@ def rank_program(g, core, T, topo):
         tt(r("t3"), r("t2"), r("e"), OP.add)
         ts(r("pl"), r("t3"), r("ckf"), None, OP.add)
         mm(r("p5", 0, 256), r("IBf"), r("e"))
-        act(r("penal"), r("p5", 0, 256), AF.Abs, scale=8192.0)
+        if t and t + 2 < STEPS:
+            own(t + 2)
         if t == 0:
             own_list(0)
             own(1)
             e_gather(0, 0)
+            act(r("penal"), r("p5", 0, 256), AF.Abs, scale=8192.0)
             d_chunk("pl", "p3", 0)
             e_minus(0, 0)
             d_chunk("PLE0", "p2", 1)
@@ -362,32 +368,33 @@ def rank_program(g, core, T, topo):
             d_chunk("pl", "p3", 2)
             d_chunk("PLE0", "p2", 3)
             own_list(1)
+            own(2)
             e_store(0)
             for k in range(STEPS):
                 act(r("stage", 128 * k, 128 * k + 128), r("R", 6 + k, COLS, 32))
                 send(frm(k), r("msg%d" % k, 0, 128), r("stage", 128 * k, 128 * k + 128), "pre%d" % k)
         else:
             e_gather(t, 3)
-            d_chunk("pl", "p3", 0)
             e_abs(2)
             e_sum(2)
             e_minus(t, 3)
+            act(r("penal"), r("p5", 0, 256), AF.Abs, scale=8192.0)
+            d_chunk("pl", "p3", 0)
             d_chunk("pl", "p3", 1)
             e_abs(3)
             e_sum(3)
             d_chunk("pl", "p3", 2)
             e_store(t)
         d_chunk("pl", "p4", 3)
+        if t + 2 < STEPS:
+            own_list(t + 2)
         if t:
             tt(r("Ep"), ("ind", r("E", 0, 256 * t + 256), r("vcL")), r("penal"), OP.add)
             tt(r("oe"), ("ind", r("O", 0, 256 * t + 256), r("vcL")), r("e"), OP.subtract)
         else:
             tt(r("Ep"), r("E", 0, 256), r("penal"), OP.add)
             tt(r("oe"), r("O", 0, 256), r("e"), OP.subtract)
-        act(r("Es"), r("Ep"), AF.Identity, bias=r("k0n"))
-        if t + 2 < STEPS:
-            own(t + 2)
-            own_list(t + 2)
+        ts(r("Es"), r("Ep"), r("k0n"), None, OP.add)
         if t + 1 < STEPS:
             e_gather(t + 1, 0)
             e_gather(t + 1, 1)
@@ -406,6 +413,8 @@ def rank_program(g, core, T, topo):
         mm(r("p5", 0, 16), r("BM"), r("incl"), False, True)
         ts(r("f256"), r("p6", 0, 16), 6.5, 256.0, OP.is_ge, OP.mult)
         ts(r("nf"), r("p6", 0, 16), 6.5, 4096.0, OP.is_lt, OP.mult)
+        if not last:
+            mm(r("p6", 64, 65), r("ones"), r("incl", 15, 16))
         tt(r("y"), r("p5", 0, 16), r("D0m"), OP.min)
         ts(r("offm"), r("y"), 1023.0, None, OP.add)
         tt(("ind", r("msg%d" % t), r("offm")), r("e"), r("prod"), OP.add)
@@ -429,7 +438,7 @@ def rank_program(g, core, T, topo):
             act(r("u"), ("ind", r("U"), r("vcL")))
             act(r(rb), ("ind", aw, r("selL")))
             for k in range(VREP, 16):
-                act(r("qrep", k, 4096, 16), r("q"))
+                gcopy(r("qrep", k, 4096, 16), r("q"))
             e_gather(t + 1, 2)
             e_abs(1)
             e_sum(1)
@@ -443,7 +452,6 @@ def rank_program(g, core, T, topo):
             act(r(rb), ("ind", aw, r("selL")))
         tt(("ind", r("R"), r("offR")), r("e"), r("prod"), OP.add)
         if not last:
-            mm(r("p6", 64, 65), r("ones"), r("incl", 15, 16))
             for k in range(VREP):
                 tc(r("qrep", k, 4096, 16), r("q"))
             tc(r("bi"), r("p6", 64, 65))
@@ -451,7 +459,7 @@ def rank_program(g, core, T, topo):
             tt(r("thb"), r("thf"), r("bj"), OP.add)
         tc(("ind", r("A"), r("offR")), r(ra))
         if t > 0:
-            act(r("yht", t - 1, 768, 6), r("land", 128 * t - 128, 128 * t))
+            gcopy(r("yht", t - 1, 768, 6), r("land", 128 * t - 128, 128 * t))
 
     store(T.yv[:], T.l3[0:128:16, :], r("vrep"))
     store(T.ya[:], T["arep%d" % (STEPS % 2)][0:128:16, :], r("arep%d" % (STEPS % 2)))

@@ -10,14 +10,15 @@ def _scratch():
             s[n] = ("sbuf", [128, w], dtype)
     sb(b, X=12288, Q=1536, qrep=4096, WK=2048, SB=2048, BM=128, rmp=128, rmBM=128, krBM=128, Ibf=128, nI=128, Gt=128,
        U2=128, ones=128, Wu=128, Ahi=256, Alo=256, df0=1024, df1=1024, df2=1024, ab0=1024, ab1=1024, Xg0=1024, Xg1=1024,
-       Ea0=1024, Ea1=1024, sf=256, fT=16, incl=16)
+       Xg2=1024, Xg3=1024, Ea0=1024, Ea1=1024, sf=256, fT=16, incl=16)
     sb(i, Ri=4096, Ab=256, Ai1=256, Ai2=256, wi=1, thi=1, pi=1, ri=256, colsi=16, rgi=128, rmi=256, ui=512,
        uj=512, t1=256, t2=256, l1=256, l2=256)
     sb(f, R=8192, A=8192, U=1536, O=1536, E=1536, VT=1792, colsf=16, B0f=128, IBf=128, I1f=128, diag=256, rz=256,
-       dup=32, dupT=32, e=256, u=256, t3=256, l3=256, penal=256, Ep=256, Es=256, oe=256, mn=256, sub=256, prod=256,
-       tile=320, am=256, sc=256, arep0=256, arep1=256, land=768, stage=768, yht=768)
+       dup=32, dupT=32, e=256, u=256, t3=256, l3=256, penal=256, Ep=256, Es=256, oe=256, mn=256, prod=256,
+       tile=320, am=256, sc=256, arep0=256, arep1=256, stage=768, yht=768)
     sb(b, q=256)
     sb(u, pl=256, aL=16, vcL=16, selL=16, offm=16, offR=16)
+    s["land"] = ("sbuf", [128, 768], f)
     for k in range(6):
         s["msg%d" % k] = ("sbuf", [128, 512], f)
         s["PLE%d" % k] = ("sbuf", [128, 256], u)
@@ -29,8 +30,14 @@ def _scratch():
 SCRATCH = _scratch()
 SEMAPHORES = (["cv", "cs", "ct", "cg", "ls", "out"] + ["ld%d" % k for k in range(9)]
               + ["pre%d" % k for k in range(6)] + ["arr%d" % k for k in range(6)])
-STEPS, LANES, COLS, CHUNK = 6, 256, 4096, 64
-VREP = 11
+STEPS, LANES, COLS = 6, 256, 4096
+VQ0 = 4
+ASPLIT = 4
+VREP, SREP = 9, 1
+FIRST = "O1 G0 P G1 M0 N0 D0 A0 B0 S0 M1 N1 V2 D1 A1 B1 S1 V3 L1 O2 D2 D3 C"
+EARLY = "G3 A2 B2 M3 N3 P D0 D1 A3 S2 B3 S3 D2 D3 C"
+TAIL = "G1 G0"
+LATE = "M0 N0 G2 A0 Q0 B0 M1 N1 S0 Q2 A1 B1 S1 M2 Q1 N2 R0"
 
 
 def rank_program(g, core, T, topo):
@@ -50,7 +57,7 @@ def rank_program(g, core, T, topo):
         small[x] = ("colsi", k, k + 1)
     for k, x in enumerate("pgf pmf odf evf pm1 ckf k0n wf thf thb".split()):
         small[x] = ("colsf", k, k + 1)
-    for k, x in enumerate("iT D0m tA tB y nf f256 dd y1 y2 y3 aT vT0 vT1 vc0 vc1".split()):
+    for k, x in enumerate("iT D0m tA tB y nf f256 dd y1 y2 y3 vT0 vT1 vc0 vc1".split()):
         small[x] = ("tile", 16 * k, 16 * k + 16)
     alias = {"yrt": "U", "yant": "E", "vrep": "l3"}
 
@@ -144,13 +151,12 @@ def rank_program(g, core, T, topo):
     def scan(out, d0, d1, op0, op1):
         emit("v", lambda: g.vector.tensor_tensor_scan(ap(out), ap(d0), ap(d1), 0.0, op0, op1), many(d0, d1), [out])
 
-    def act(out, in_, func=AF.Copy, scale=None, bias=None):
-        kw = {}
-        if scale is not None:
-            kw["scale"] = ap(scale)
-        if bias is not None:
-            kw["bias"] = ap(bias)
-        emit("s", lambda: g.scalar.activation(ap(out), ap(in_), func, **kw), many(in_, scale, bias), [out])
+    def act(out, in_, func=AF.Copy, scale=None):
+        kw = {} if scale is None else {"scale": scale}
+        emit("s", lambda: g.scalar.activation(ap(out), ap(in_), func, **kw), many(in_), [out])
+
+    def pick(out, in_, pattern, base):
+        emit("g", lambda: g.affine_select(ap(out), ap(in_), pattern, OP.is_equal, 0.0, base, 0), [in_], [out])
 
     def gcopy(out, in_):
         k = len(range(out[1], out[2], out[3]))
@@ -196,15 +202,15 @@ def rank_program(g, core, T, topo):
     load("ld1", r("wi"), T.w[:])
     load("ld2", r("thi"), T.th[:])
     load("ld3", r("X", 0, COLS), T.xc[:])
-    for k in range(4):
-        load("ld%d" % (4 + k), r("Ri", 1024 * k, 1024 * k + 1024), T.rf[:, 1024 * k:1024 * k + 1024])
+    pieces = ((0, 1024), (1024, 2048), (2048, 3072), (3072, 3584), (3584, COLS))
+    for k, (a, b) in enumerate(pieces):
+        load("ld%d" % (4 + k), r("Ri", a, b), T.rf[:, a:b])
     for t in range(STEPS):
         will_land(r("msg%d" % t, 0, 128), "pre%d" % t, to(t))
         will_land(r("land", 128 * t, 128 * t + 128), "arr%d" % t, frm(t))
 
     iota(r("pi"), [[0, 1]], 0, 1)
     iota(r("ri"), [[1, 256]], 0, 0)
-    iota(r("VT"), [[1, 7], [16, 256]], 0, 0, True)
     fill(r("ones"), 1.0)
     ts(r("pgi"), r("pi"), 4, None, OP.arith_shift_right)
     ts(r("pmi"), r("pi"), 15, None, OP.bitwise_and)
@@ -226,15 +232,19 @@ def rank_program(g, core, T, topo):
     tc(r("Alo"), r("Ai2"))
     for k in range(16):
         ts(r("SB", 128 * k, 128 * k + 128), r("krBM"), float(k + 1), None, OP.is_equal)
-    for k in range(16):
+
+    def spread(k):
         bank = ("p0", "p1", "p3", "p4")[k // 2 % 4]
         x = r(bank, 256 * (k % 2), 256 * (k % 2) + 256)
         mm(x, r("SB", 128 * k, 128 * k + 128), r("Ahi"), True, False)
         mm(x, r("SB", 128 * k, 128 * k + 128), r("Alo"), False, True)
         if k % 2:
             act(r("A", 256 * k - 256, 256 * k + 256), r(bank))
+
+    for k in range(2 * ASPLIT):
+        spread(k)
     for k in range(16):
-        ts(r("WK", 128 * k, 128 * k + 128), r("rmBM"), float(k + 1), None, OP.is_equal)
+        pick(r("WK", 128 * k, 128 * k + 128), r("BM"), [[0, 8], [1, 16]], -k)
     tc(r("dup", 0, 16), r("Ab", 0, 256, 16))
     tc(r("dup", 16, 32), r("Ab", 0, 256, 16))
     ts(r("Ibf"), r("rmBM"), r("pm1"), None, OP.is_equal)
@@ -244,9 +254,9 @@ def rank_program(g, core, T, topo):
     ts(r("tA"), r("dupT", 0, 16), r("evf"), None, OP.mult)
     ts(r("tB"), r("dupT", 16, 32), r("odf"), None, OP.mult)
     tt(r("Gt"), r("Gt"), r("BM"), OP.mult)
-    tt(r("aT"), r("tA"), r("tB"), OP.add)
+    tt(r("sc", 15, 256, 16), r("tA"), r("tB"), OP.add)
     tt(r("U2"), r("I1f"), r("Gt"), OP.subtract)
-    tc(r("aL"), r("aT"))
+    tc(r("aL"), r("sc", 15, 256, 16))
     ts(r("nI"), r("Ibf"), -1.0, None, OP.mult)
     tc(r("B0f"), r("SB", 0, 128))
     tt(r("IBf"), r("Ibf"), r("SB", 0, 128), OP.subtract)
@@ -264,10 +274,11 @@ def rank_program(g, core, T, topo):
     tc(r("thf"), r("thi"))
     ts(r("Wu"), r("BM"), r("wf"), None, OP.mult)
     tc(r("thb"), r("thi"))
-    act(r("arep0"), r("A", 0, COLS, 16))
 
     for s in range(STEPS):
-        tc(r("Q", 256 * s, 256 * s + 256), r("X", s, COLS, 16))
+        (tc if s < 2 else act)(r("Q", 256 * s, 256 * s + 256), r("X", s, COLS, 16))
+    gcopy(r("X", 4096, 8192), r("X", 0, COLS))
+    iota(r("VT"), [[1, 7], [16, 256]], 0, 0, True)
     act(r("X", 8192, 12288), r("X", 0, COLS))
     for h in range(3):
         bank = ("p2", "p5", "p6")[h]
@@ -279,10 +290,18 @@ def rank_program(g, core, T, topo):
         tc(r("U", 512 * h, 512 * h + 512), r("uj"))
         if h == 0:
             for k in range(16):
-                tc(r("qrep", k, 4096, 16), r("Q", 0, 256))
-    tc(r("X", 4096, 8192), r("X", 0, COLS))
-    for k in range(4):
-        tc(r("R", 1024 * k, 1024 * k + 1024), r("Ri", 1024 * k, 1024 * k + 1024))
+                if k < VQ0:
+                    tc(r("qrep", k, 4096, 16), r("Q", 0, 256))
+                else:
+                    act(r("qrep", k, 4096, 16), r("Q", 0, 256))
+    for k in range(2 * ASPLIT, 16):
+        spread(k)
+    act(r("arep0"), r("A", 0, COLS, 16))
+    for a, b in pieces:
+        tc(r("R", a, b), r("Ri", a, b))
+    for k in range(STEPS):
+        gcopy(r("stage", 128 * k, 128 * k + 128), r("R", 6 + k, COLS, 32))
+        send(frm(k), r("msg%d" % k, 0, 128), r("stage", 128 * k, 128 * k + 128), "pre%d" % k)
 
     def own(s):
         mm(r("p7", 0, 256), r("B0f"), r("R", s, COLS, 16))
@@ -292,48 +311,66 @@ def rank_program(g, core, T, topo):
         tt(r("l1"), x, r("U", 256 * s, 256 * s + 256), OP.mult)
         ts(r("l2"), r("l1"), 5, 4095, OP.arith_shift_right, OP.bitwise_and)
         tt(r("l3"), r("l2"), x, OP.add)
-        ts(r("PLE%d" % s), r("l3"), r("ckf"), None, OP.add)
         tc(r("O", 256 * s, 256 * s + 256), x)
+        ts(r("PLE%d" % s), r("l3"), r("ckf"), None, OP.add)
 
     def e_gather(s, p):
-        act(r("Xg%d" % (p % 2)), ("ind", r("X"), r("PLE%d" % s, 64 * p, 64 * p + 64)))
+        act(r("Xg%d" % p), ("ind", r("X"), r("PLE%d" % s, 64 * p, 64 * p + 64)))
 
-    def e_minus(s, p):
-        for k in range(16):
-            x = r("p%d" % (k // 8), 64 * (k % 8), 64 * (k % 8) + 64)
-            mm(x, r("Ibf"), r("Xg%d" % (p % 2), k, 1024, 16), True, False)
+    def e_minus(s, p, h):
+        for k in range(8 * h, 8 * h + 8):
+            x = r("p%d" % h, 64 * (k % 8), 64 * (k % 8) + 64)
+            mm(x, r("Ibf"), r("Xg%d" % p, k, 1024, 16), True, False)
             mm(x, r("nI"), r("Q", 256 * s + 64 * p, 256 * s + 64 * p + 64), False, True)
 
-    def e_abs(p):
-        for h in range(2):
-            act(r("Ea%d" % (p % 2), 512 * h, 512 * h + 512), r("p%d" % h), AF.Abs)
+    def e_abs(p, h):
+        act(r("Ea%d" % (p % 2), 512 * h, 512 * h + 512), r("p%d" % h), AF.Abs)
 
     def e_sum(p):
         for k in range(16):
             mm(r("p2", 64 * p, 64 * p + 64), r("WK", 128 * k, 128 * k + 128),
                r("Ea%d" % (p % 2), 64 * k, 64 * k + 64), k == 0, k == 15)
 
-    def e_store(s):
-        act(r("E", 256 * s, 256 * s + 256), r("p2", 0, 256))
-
-    def d_gather(lst, c, b):
-        tt(r("df%d" % b), ("ind", r("X"), r(lst, 64 * c, 64 * c + 64)), r("qrep", 1024 * c, 1024 * c + 1024), OP.subtract)
-
-    def d_abs(b, b2):
-        act(r("ab%d" % b2), r("df%d" % b), AF.Abs)
-
-    def d_sum(bank, c, b2):
-        for k in range(16):
-            mm(r(bank, 64 * c, 64 * c + 64), r("WK", 128 * k, 128 * k + 128), r("ab%d" % b2, k, 1024, 16), k == 0, k == 15)
-
-    nbuf = [0, 0]
+    nbuf = [0]
 
     def d_chunk(lst, bank, c):
-        b, b2 = nbuf[0] % 3, nbuf[0] % 2
+        df, ab = "df%d" % (nbuf[0] % 3), "ab%d" % (nbuf[0] % 2)
         nbuf[0] += 1
-        d_gather(lst, c, b)
-        d_abs(b, b2)
-        d_sum(bank, c, b2)
+        tt(r(df), ("ind", r("X"), r(lst, 64 * c, 64 * c + 64)), r("qrep", 1024 * c, 1024 * c + 1024), OP.subtract)
+        act(r(ab), r(df), AF.Abs)
+        for k in range(16):
+            mm(r(bank, 64 * c, 64 * c + 64), r("WK", 128 * k, 128 * k + 128), r(ab, k, 1024, 16), k == 0, k == 15)
+
+    def work(plan, s, gathers=()):
+        for x in plan.split():
+            k = int(x[1:] or 0)
+            if x[0] == "G":
+                e_gather(s, k)
+            elif x[0] in "MN":
+                e_minus(s, k, int(x[0] == "N"))
+            elif x[0] in "AB":
+                e_abs(k, int(x[0] == "B"))
+            elif x[0] == "S":
+                e_sum(k)
+            elif x[0] == "C":
+                act(r("E", 256 * s, 256 * s + 256), r("p2", 0, 256))
+            elif x[0] == "D":
+                d_chunk("pl", "p4" if k == 3 else "p3", k)
+            elif x[0] == "V":
+                d_chunk("PLE%d" % s, "p2", k)
+            elif x[0] == "P":
+                act(r("penal"), r("p5", 0, 256), AF.Abs, scale=8192.0)
+            elif x[0] == "O":
+                own(k)
+            elif x[0] == "L":
+                own_list(k)
+            elif x[0] == "Q":
+                act(r(gathers[k][0]), gathers[k][1])
+                if k == 0:
+                    for j in range(VREP + SREP, 16):
+                        gcopy(r("qrep", j, 4096, 16), r("q"))
+            elif x[0] == "R":
+                act(r("qrep", VREP + k, 4096, 16), r("q"))
 
     own(0)
     for t in range(STEPS):
@@ -341,51 +378,27 @@ def rank_program(g, core, T, topo):
         va, vb = "vT%d" % (t % 2), "vT%d" % ((t + 1) % 2)
         ca, cb = "vc%d" % (t % 2), "vc%d" % ((t + 1) % 2)
         ra, rb = "arep%d" % (t % 2), "arep%d" % ((t + 1) % 2)
-        rw = r("R", 0, COLS)
+        rw, aw = r("R", 0, COLS), r("A", 0, COLS)
+        aT = r("sc", 15, 256, 16)
         if t > 0:
             tc(r("R", 6 + t - 1, COLS, 32), r("land", 128 * t - 128, 128 * t))
         act(r("e"), ("ind", rw, r("aL")))
         u = r("u") if t else r("U", 0, 256)
-        tt(r("t1"), ("ind", rw, r("aL")), u, OP.mult)
-        ts(r("t2"), r("t1"), 5, 4095, OP.arith_shift_right, OP.bitwise_and)
-        tt(r("t3"), r("t2"), r("e"), OP.add)
-        ts(r("pl"), r("t3"), r("ckf"), None, OP.add)
+        two = ((0, 128), (128, 256))
+        for a, b in two:
+            tt(r("t1", a, b), ("ind", rw, r("aL", a // 16, b // 16)), (u[0], a, b, 1), OP.mult)
+        for a, b in two:
+            ts(r("t2", a, b), r("t1", a, b), 5, 4095, OP.arith_shift_right, OP.bitwise_and)
+        for a, b in two:
+            tt(r("t3", a, b), r("t2", a, b), r("e", a, b), OP.add)
+        for a, b in two:
+            ts(r("pl", a, b), r("t3", a, b), r("ckf"), None, OP.add)
         mm(r("p5", 0, 256), r("IBf"), r("e"))
         if t and t + 2 < STEPS:
             own(t + 2)
         if t == 0:
             own_list(0)
-            own(1)
-            e_gather(0, 0)
-            act(r("penal"), r("p5", 0, 256), AF.Abs, scale=8192.0)
-            d_chunk("pl", "p3", 0)
-            e_minus(0, 0)
-            d_chunk("PLE0", "p2", 1)
-            e_abs(0)
-            e_sum(0)
-            d_chunk("pl", "p3", 1)
-            d_chunk("PLE0", "p2", 2)
-            d_chunk("pl", "p3", 2)
-            d_chunk("PLE0", "p2", 3)
-            own_list(1)
-            own(2)
-            e_store(0)
-            for k in range(STEPS):
-                act(r("stage", 128 * k, 128 * k + 128), r("R", 6 + k, COLS, 32))
-                send(frm(k), r("msg%d" % k, 0, 128), r("stage", 128 * k, 128 * k + 128), "pre%d" % k)
-        else:
-            e_gather(t, 3)
-            e_abs(2)
-            e_sum(2)
-            e_minus(t, 3)
-            act(r("penal"), r("p5", 0, 256), AF.Abs, scale=8192.0)
-            d_chunk("pl", "p3", 0)
-            d_chunk("pl", "p3", 1)
-            e_abs(3)
-            e_sum(3)
-            d_chunk("pl", "p3", 2)
-            e_store(t)
-        d_chunk("pl", "p4", 3)
+        work(FIRST if t == 0 else EARLY, t)
         if t + 2 < STEPS:
             own_list(t + 2)
         if t:
@@ -394,19 +407,18 @@ def rank_program(g, core, T, topo):
         else:
             tt(r("Ep"), r("E", 0, 256), r("penal"), OP.add)
             tt(r("oe"), r("O", 0, 256), r("e"), OP.subtract)
-        ts(r("Es"), r("Ep"), r("k0n"), None, OP.add)
-        if t + 1 < STEPS:
-            e_gather(t + 1, 0)
-            e_gather(t + 1, 1)
-        x0, x1 = (0, 192), (192, 256)
-        for (a, b), bank in ((x0, "p3"), (x1, "p4")):
+        if not last:
+            work(TAIL, t + 1)
+        halves = ((0, 192, "p3"), (192, LANES, "p4"))
+        for a, b, bank in halves:
             tt(r("mn", a, b), r("Ep", a, b), r(bank, a, b), OP.min)
             ts(r("sf", a, b), r("mn", a, b), r("thb"), None, OP.is_lt)
         for k in range(16):
             mm(r("p6", 0, 16), r("WK", 128 * k, 128 * k + 128), r("sf", k, 256, 16), k == 0, k == 15)
-        for (a, b), bank in ((x0, "p3"), (x1, "p4")):
-            tt(r("sub", a, b), r("Es", a, b), r(bank, a, b), OP.is_lt)
-        tt(r("prod"), r("sub"), r("oe"), OP.mult)
+        ts(r("Es"), r("Ep"), r("k0n"), None, OP.add)
+        for a, b, bank in halves:
+            tt(r("p7", 256 + a, 256 + b), r("Es", a, b), r(bank, a, b), OP.is_lt)
+        tt(r("prod"), r("p7", 256, 512), r("oe"), OP.mult)
         ts(r("fT"), r("p6", 0, 16), 6.5, None, OP.is_ge)
         scan(r("incl"), r("ones", 0, 16), r("fT"), OP.mult, OP.add)
         mm(r("p5", 0, 16), r("U2"), r("fT"), True, False)
@@ -422,59 +434,49 @@ def rank_program(g, core, T, topo):
         tt(r(cb), r(ca), r("f256"), OP.add)
         tt(r(vb), r(va), r("fT"), OP.add)
         tc(r("vcL"), r(cb))
-        tt(r("dd"), r(vb), r("aT"), OP.subtract)
+        tt(r("dd"), r(vb), aT, OP.subtract)
         tt(r("y1"), r("dd"), r("fT"), OP.mult)
         tt(r("y3"), r("nf"), r(va), OP.add)
-        tt(r("y2"), r("y1"), r("aT"), OP.add)
+        tt(r("y2"), r("y1"), aT, OP.add)
         tc(r("offR"), r("y3"))
         tc(r("selL"), r("y2"))
-        aw = r("A", 0, COLS)
-        if t + 1 < STEPS:
-            e_minus(t + 1, 0)
-            e_abs(0)
-            e_sum(0)
-            e_minus(t + 1, 1)
-            act(r("q"), ("ind", r("Q"), r("vcL")))
-            act(r("u"), ("ind", r("U"), r("vcL")))
-            act(r(rb), ("ind", aw, r("selL")))
-            for k in range(VREP, 16):
-                gcopy(r("qrep", k, 4096, 16), r("q"))
-            e_gather(t + 1, 2)
-            e_abs(1)
-            e_sum(1)
-            e_minus(t + 1, 2)
+        if not last:
+            work(LATE, t + 1, [("q", ("ind", r("Q"), r("vcL"))), ("u", ("ind", r("U"), r("vcL"))), (rb, ("ind", aw, r("selL")))])
             tt(r("am"), ("ind", aw, r("selL")), r("diag"), OP.mult)
-            scan(r("sc"), r("rz"), r("am"), OP.mult, OP.add)
-            tc(r("aL"), r("sc", 15, 256, 16))
-            tc(r("aT"), r("sc", 15, 256, 16))
         else:
             act(r("vrep"), ("ind", r("VT"), r("vcL")))
             act(r(rb), ("ind", aw, r("selL")))
         tt(("ind", r("R"), r("offR")), r("e"), r("prod"), OP.add)
         if not last:
+            scan(r("sc"), r("rz"), r("am"), OP.mult, OP.add)
+            tc(r("bi"), r("p6", 64, 65))
             for k in range(VREP):
                 tc(r("qrep", k, 4096, 16), r("q"))
-            tc(r("bi"), r("p6", 64, 65))
-            ts(r("bj"), r("bi"), 255, None, OP.bitwise_and)
-            tt(r("thb"), r("thf"), r("bj"), OP.add)
+                if k == 1:
+                    tc(r("aL"), aT)
+                if k == 3:
+                    ts(r("bj"), r("bi"), 255, None, OP.bitwise_and)
+                if k == 5:
+                    tt(r("thb"), r("thf"), r("bj"), OP.add)
+        if last:
+            for s in range(3):
+                act(r("p%d" % s, 0, 256), r("R", 3 + s, COLS, 16), AF.Copy, scale=4096.0)
+                tt(r("yrt", s, 768, 3), r("p%d" % s, 0, 256), r("R", s, COLS, 16), OP.add)
         tc(("ind", r("A"), r("offR")), r(ra))
         if t > 0:
-            gcopy(r("yht", t - 1, 768, 6), r("land", 128 * t - 128, 128 * t))
+            gcopy(r("yht", t - 1, 768, 6), r("R", 6 + t - 1, COLS, 32))
 
     store(T.yv[:], T.l3[0:128:16, :], r("vrep"))
     store(T.ya[:], T["arep%d" % (STEPS % 2)][0:128:16, :], r("arep%d" % (STEPS % 2)))
-    for s in range(3):
-        act(r("p%d" % s, 0, 256), r("R", 3 + s, COLS, 16), AF.Copy, scale=4096.0)
-        tt(r("yrt", s, 768, 3), r("p%d" % s, 0, 256), r("R", s, COLS, 16), OP.add)
     store(T.yr[:], T.U[:, 0:768], r("yrt", 0, 768))
+    tc(r("yht", STEPS - 1, 768, 6), r("land", 128 * STEPS - 128, 128 * STEPS))
+    store(T.yh[:], T.yht[:], r("yht"))
     for s in range(6):
-        if s % 2:
+        if s != 5:
             act(r("yant", s, 1536, 6), r("A", s, COLS, 16))
         else:
             tc(r("yant", s, 1536, 6), r("A", s, COLS, 16))
     store(T.yan[:], T.E[0:128:16, :], r("yant"))
-    tc(r("yht", STEPS - 1, 768, 6), r("land", 128 * STEPS - 128, 128 * STEPS))
-    store(T.yh[:], T.yht[:], r("yht"))
     for sem in ("cv", "cs", "ct", "cg"):
         wait("g", sem, count[sem])
     g.wait_ge(T.sem["ls"], sent[0])

import math
from concourse.mybir import AluOpType as OP, ActivationFunctionType as AF


def _scratch():
    f, b, i, u = "float32", "bfloat16", "int32", "uint16"
    s = {}
    def sb(dtype, **kw):
        for n, w in kw.items():
            s[n] = ("sbuf", [128, w], dtype)
    sb(b, X=12288, Q=1536, qrep=4096, WK=2048, SB=2048, BM=128, rmp=128, rmBM=128, krBM=128, Ibf=128, nI=128, Gt=128,
       U2=128, ones=128, Wu=128, Ahi=256, Alo=256, df0=1024, df1=1024, df2=1024, ab0=1024, ab1=1024, Xg0=1024, Xg1=1024,
       Xg2=1024, Xg3=1024, Ea0=1024, Ea1=1024, sf=256, fT=16, incl=16)
    sb(i, Ri=4096, Ab=256, Ai1=256, Ai2=256, wi=1, thi=1, pi=1, ri=256, colsi=16, rgi=128, rmi=256, ui=512,
       uj=512, t1=256, t2=256, l1=256, l2=256)
    sb(f, R=8192, A=8192, U=1536, O=1536, E=1536, VT=1792, colsf=16, B0f=128, IBf=128, I1f=128, diag=256, rz=256,
       dup=32, dupT=32, e=256, u=256, t3=256, l3=256, penal=256, Ep=256, Es=256, oe=256, mn=256, prod=256,
       tile=320, am=256, sc=256, arep0=256, arep1=256, stage=768, yht=768)
    sb(b, q=256)
    sb(u, pl=256, aL=16, vcL=16, selL=16, offm=16, offR=16)
    s["land"] = ("sbuf", [128, 768], f)
    for k in range(6):
        s["msg%d" % k] = ("sbuf", [128, 512], f)
        s["PLE%d" % k] = ("sbuf", [128, 256], u)
    for k in range(8):
        s["p%d" % k] = ("psum", [128, 512], f)
    return s


SCRATCH = _scratch()
SEMAPHORES = (["cv", "cs", "ct", "cg", "ls", "out"] + ["ld%d" % k for k in range(9)]
              + ["pre%d" % k for k in range(6)] + ["arr%d" % k for k in range(6)])
STEPS, LANES, COLS = 6, 256, 4096
VQ0 = 4
ASPLIT = 4
VREP, SREP = 9, 1
FIRST = "O1 G0 P G1 M0 N0 D0 A0 B0 S0 M1 N1 V2 D1 A1 B1 S1 V3 L1 O2 D2 D3 C"
EARLY = "G3 A2 B2 M3 N3 P D0 D1 A3 S2 B3 S3 D2 D3 C"
TAIL = "G1 G0"
LATE = "M0 N0 G2 A0 Q0 B0 M1 N1 S0 Q2 A1 B1 S1 M2 Q1 N2 R0"


def rank_program(g, core, T, topo):
    rank = T.rank_of(core)
    if rank is None:
        return
    cores, n = T.cores, len(T.cores)
    eng = {"v": g.vector, "s": g.scalar, "t": g.tensor, "g": g, "y": g.sync}
    qsem = {"v": "cv", "s": "cs", "t": "ct", "g": "cg"}
    count = {"cv": 0, "cs": 0, "ct": 0, "cg": 0}
    known = {q: {} for q in eng}
    clock = {}
    hist = {}

    small = {}
    for k, x in enumerate("pgi pmi odi cki bi bj".split()):
        small[x] = ("colsi", k, k + 1)
    for k, x in enumerate("pgf pmf odf evf pm1 ckf k0n wf thf thb".split()):
        small[x] = ("colsf", k, k + 1)
    for k, x in enumerate("iT D0m tA tB y nf f256 dd y1 y2 y3 vT0 vT1 vc0 vc1".split()):
        small[x] = ("tile", 16 * k, 16 * k + 16)
    alias = {"yrt": "U", "yant": "E", "vrep": "l3"}

    def r(name, a=0, b=None, step=1):
        if name in small:
            return small[name] + (1,)
        name = alias.get(name, name)
        return (name, a, SCRATCH[name][1][1] if b is None else b, step)

    def ap(x):
        if not isinstance(x, tuple):
            return x
        if x[0] == "ind":
            return ap(x[1]).indirect(ap(x[2]))
        return T[x[0]][:, x[1]:x[2]] if x[3] == 1 else T[x[0]][:, x[1]:x[2]:x[3]]

    def parts(x):
        if not isinstance(x, tuple):
            return []
        return [x[1], x[2]] if x[0] == "ind" else [x]

    def meet(x, y):
        return x[1] < y[2] and y[1] < x[2] and (x[1] - y[1]) % math.gcd(x[3], y[3]) == 0

    def covers(x, y):
        return x[1:] == y[1:] or (x[3] == 1 and x[1] <= y[1] and x[2] >= y[2])

    def wait(q, sem, val):
        if known[q].get(sem, 0) >= val:
            return
        eng[q].wait_ge(T.sem[sem], val)
        for s, v in list(clock.get((sem, val), {}).items()) + [(sem, val)]:
            known[q][s] = max(known[q].get(s, 0), v)

    def order(q, reads, writes, inner=False):
        need = {}
        for regs, w in ((reads, False), (writes, True)):
            for x in regs:
                psum = SCRATCH[x[0]][0] == "psum"
                for y, yw, yq, sem, val in hist.get(x[0], []):
                    if psum and yq != q:
                        hit = True
                    else:
                        hit = (w or yw) and meet(x, y) and not (inner and yq == q)
                    if hit:
                        need[sem] = max(need.get(sem, 0), val)
        for sem in sorted(need):
            wait(q, sem, need[sem])

    def note(q, reads, writes, sem, val):
        for regs, w in ((reads, False), (writes, True)):
            for x in regs:
                h = hist.setdefault(x[0], [])
                if w:
                    h[:] = [z for z in h if not covers(x, z[0])]
                else:
                    h[:] = [z for z in h if z[1] or z[2] != q or not covers(x, z[0])]
                h.append((x, w, q, sem, val))

    def emit(q, call, reads, writes, inner=False):
        order(q, reads, writes, inner)
        sem = qsem[q]
        count[sem] += 1
        call().then_inc(T.sem[sem], 1)
        clock[(sem, count[sem])] = dict(known[q])
        note(q, reads, writes, sem, count[sem])

    def many(*xs):
        return [y for x in xs for y in parts(x)]

    def outs(x):
        return ([x[1]], [x[2]]) if x[0] == "ind" else ([x], [])

    def tt(out, in0, in1, op):
        w, o = outs(out)
        emit("v", lambda: g.vector.tensor_tensor(ap(out), ap(in0), ap(in1), op), many(in0, in1) + o, w)

    def ts(out, in0, s1, s2, op0, op1=None):
        if op1 is None:
            emit("v", lambda: g.vector.tensor_scalar(ap(out), ap(in0), ap(s1), None, op0), many(in0, s1), [out])
        else:
            emit("v", lambda: g.vector.tensor_scalar(ap(out), ap(in0), ap(s1), ap(s2), op0, op1), many(in0, s1, s2), [out])

    def tc(out, in_):
        w, o = outs(out)
        emit("v", lambda: g.vector.tensor_copy(ap(out), ap(in_)), many(in_) + o, w)

    def fill(out, value):
        emit("v", lambda: g.vector.memset(ap(out), value), [], [out])

    def scan(out, d0, d1, op0, op1):
        emit("v", lambda: g.vector.tensor_tensor_scan(ap(out), ap(d0), ap(d1), 0.0, op0, op1), many(d0, d1), [out])

    def act(out, in_, func=AF.Copy, scale=None):
        kw = {} if scale is None else {"scale": scale}
        emit("s", lambda: g.scalar.activation(ap(out), ap(in_), func, **kw), many(in_), [out])

    def pick(out, in_, pattern, base):
        emit("g", lambda: g.affine_select(ap(out), ap(in_), pattern, OP.is_equal, 0.0, base, 0), [in_], [out])

    def gcopy(out, in_):
        k = len(range(out[1], out[2], out[3]))
        emit("g", lambda: g.affine_select(ap(out), ap(in_), [[0, k]], OP.is_ge, 0.0, 0, 0), [in_], [out])

    def mm(out, lhsT, rhs, start=True, stop=True):
        emit("t", lambda: g.tensor.matmul(ap(out), ap(lhsT), ap(rhs), start, stop), many(lhsT, rhs), [out], inner=not start)

    def iota(out, pattern, base, cm, flag=False):
        if flag:
            emit("g", lambda: g.iota(ap(out), pattern, base, cm, allow_small_or_imprecise_dtypes=True), [], [out])
        else:
            emit("g", lambda: g.iota(ap(out), pattern, base, cm), [], [out])

    def load(sem, out, src):
        g.sync.dma_start(ap(out), src).then_inc(T.sem[sem], 16)
        note("y", [], [out], sem, 16)

    def store(out, src, x):
        order("y", [x], [])
        g.sync.dma_start(out, src).then_inc(T.sem["out"], 16)
        stores[0] += 16

    stores = [0]
    sent = [0]

    def send(dst, out, in_, sem):
        order("g", [in_], [])
        rid, pid, _ = topo.addr(dst)
        g.remote_dma(ap(out), ap(in_), T.sem[sem], T.sem["ls"], pid, rid, topo.mask(core, dst))
        sent[0] += len(topo.engines(core, dst))

    def will_land(x, sem, src):
        note("x", [], [x], sem, len(topo.engines(src, core)))

    def to(t):
        return cores[(rank + 1 + t % (n - 1)) % n]

    def frm(t):
        return cores[(rank - 1 - t % (n - 1)) % n]

    load("ld0", r("Ab"), T.an[:])
    load("ld1", r("wi"), T.w[:])
    load("ld2", r("thi"), T.th[:])
    load("ld3", r("X", 0, COLS), T.xc[:])
    pieces = ((0, 1024), (1024, 2048), (2048, 3072), (3072, 3584), (3584, COLS))
    for k, (a, b) in enumerate(pieces):
        load("ld%d" % (4 + k), r("Ri", a, b), T.rf[:, a:b])
    for t in range(STEPS):
        will_land(r("msg%d" % t, 0, 128), "pre%d" % t, to(t))
        will_land(r("land", 128 * t, 128 * t + 128), "arr%d" % t, frm(t))

    iota(r("pi"), [[0, 1]], 0, 1)
    iota(r("ri"), [[1, 256]], 0, 0)
    fill(r("ones"), 1.0)
    ts(r("pgi"), r("pi"), 4, None, OP.arith_shift_right)
    ts(r("pmi"), r("pi"), 15, None, OP.bitwise_and)
    ts(r("rgi"), r("ri", 0, 128), 4, None, OP.arith_shift_right)
    ts(r("rmi"), r("ri"), 15, None, OP.bitwise_and)
    ts(r("odi"), r("pgi"), 1, None, OP.bitwise_and)
    tc(r("pgf"), r("pgi"))
    tc(r("pmf"), r("pmi"))
    tc(r("odf"), r("odi"))
    ts(r("BM"), r("rgi"), r("pgf"), None, OP.is_equal)
    ts(r("rmp"), r("rmi", 0, 128), 1.0, None, OP.add)
    ts(r("pm1"), r("pmf"), 1.0, None, OP.add)
    ts(r("evf"), r("odf"), -1.0, 1.0, OP.mult, OP.add)
    tt(r("rmBM"), r("rmp"), r("BM"), OP.mult)
    ts(r("krBM"), r("BM"), r("pm1"), None, OP.mult)
    ts(r("Ai1"), r("Ab"), 4032, None, OP.bitwise_and)
    ts(r("Ai2"), r("Ab"), 63, None, OP.bitwise_and)
    tc(r("Ahi"), r("Ai1"))
    tc(r("Alo"), r("Ai2"))
    for k in range(16):
        ts(r("SB", 128 * k, 128 * k + 128), r("krBM"), float(k + 1), None, OP.is_equal)

    def spread(k):
        bank = ("p0", "p1", "p3", "p4")[k // 2 % 4]
        x = r(bank, 256 * (k % 2), 256 * (k % 2) + 256)
        mm(x, r("SB", 128 * k, 128 * k + 128), r("Ahi"), True, False)
        mm(x, r("SB", 128 * k, 128 * k + 128), r("Alo"), False, True)
        if k % 2:
            act(r("A", 256 * k - 256, 256 * k + 256), r(bank))

    for k in range(2 * ASPLIT):
        spread(k)
    for k in range(16):
        pick(r("WK", 128 * k, 128 * k + 128), r("BM"), [[0, 8], [1, 16]], -k)
    tc(r("dup", 0, 16), r("Ab", 0, 256, 16))
    tc(r("dup", 16, 32), r("Ab", 0, 256, 16))
    ts(r("Ibf"), r("rmBM"), r("pm1"), None, OP.is_equal)
    emit("v", lambda: g.vector.transpose(ap(r("dupT")), ap(r("dup"))), [r("dup")], [r("dupT")])
    ts(r("Gt"), r("rmBM"), r("pm1"), None, OP.is_le)
    ts(r("I1f"), r("Ibf"), -1023.0, None, OP.mult)
    ts(r("tA"), r("dupT", 0, 16), r("evf"), None, OP.mult)
    ts(r("tB"), r("dupT", 16, 32), r("odf"), None, OP.mult)
    tt(r("Gt"), r("Gt"), r("BM"), OP.mult)
    tt(r("sc", 15, 256, 16), r("tA"), r("tB"), OP.add)
    tt(r("U2"), r("I1f"), r("Gt"), OP.subtract)
    tc(r("aL"), r("sc", 15, 256, 16))
    ts(r("nI"), r("Ibf"), -1.0, None, OP.mult)
    tc(r("B0f"), r("SB", 0, 128))
    tt(r("IBf"), r("Ibf"), r("SB", 0, 128), OP.subtract)
    ts(r("diag"), r("rmi"), r("pmf"), None, OP.is_equal)
    ts(r("rz"), r("rmi"), 0.5, None, OP.is_gt)
    ts(r("iT"), r("ri", 0, 16), 16.0, r("pmf"), OP.mult, OP.add)
    ts(r("cki"), r("pmf"), 613.0, None, OP.mult)
    ts(r("k0n"), r("pmf"), 0.5, -1000000.0, OP.is_lt, OP.mult)
    ts(r("vT0"), r("iT"), 16.0, None, OP.mult)
    ts(r("cki"), r("cki"), 4095, None, OP.bitwise_and)
    tc(r("vc0"), r("iT"))
    ts(r("D0m"), r("iT"), -767.0, None, OP.add)
    tc(r("ckf"), r("cki"))
    tc(r("wf"), r("wi"))
    tc(r("thf"), r("thi"))
    ts(r("Wu"), r("BM"), r("wf"), None, OP.mult)
    tc(r("thb"), r("thi"))

    for s in range(STEPS):
        (tc if s < 2 else act)(r("Q", 256 * s, 256 * s + 256), r("X", s, COLS, 16))
    gcopy(r("X", 4096, 8192), r("X", 0, COLS))
    iota(r("VT"), [[1, 7], [16, 256]], 0, 0, True)
    act(r("X", 8192, 12288), r("X", 0, COLS))
    for h in range(3):
        bank = ("p2", "p5", "p6")[h]
        mm(r(bank), r("Wu"), r("Q", 512 * h, 512 * h + 512))
    for h in range(3):
        bank = ("p2", "p5", "p6")[h]
        tc(r("ui"), r(bank))
        ts(r("uj"), r("ui"), 4095, None, OP.bitwise_and)
        tc(r("U", 512 * h, 512 * h + 512), r("uj"))
        if h == 0:
            for k in range(16):
                if k < VQ0:
                    tc(r("qrep", k, 4096, 16), r("Q", 0, 256))
                else:
                    act(r("qrep", k, 4096, 16), r("Q", 0, 256))
    for k in range(2 * ASPLIT, 16):
        spread(k)
    act(r("arep0"), r("A", 0, COLS, 16))
    for a, b in pieces:
        tc(r("R", a, b), r("Ri", a, b))
    for k in range(STEPS):
        gcopy(r("stage", 128 * k, 128 * k + 128), r("R", 6 + k, COLS, 32))
        send(frm(k), r("msg%d" % k, 0, 128), r("stage", 128 * k, 128 * k + 128), "pre%d" % k)

    def own(s):
        mm(r("p7", 0, 256), r("B0f"), r("R", s, COLS, 16))

    def own_list(s):
        x = r("p7", 0, 256)
        tt(r("l1"), x, r("U", 256 * s, 256 * s + 256), OP.mult)
        ts(r("l2"), r("l1"), 5, 4095, OP.arith_shift_right, OP.bitwise_and)
        tt(r("l3"), r("l2"), x, OP.add)
        tc(r("O", 256 * s, 256 * s + 256), x)
        ts(r("PLE%d" % s), r("l3"), r("ckf"), None, OP.add)

    def e_gather(s, p):
        act(r("Xg%d" % p), ("ind", r("X"), r("PLE%d" % s, 64 * p, 64 * p + 64)))

    def e_minus(s, p, h):
        for k in range(8 * h, 8 * h + 8):
            x = r("p%d" % h, 64 * (k % 8), 64 * (k % 8) + 64)
            mm(x, r("Ibf"), r("Xg%d" % p, k, 1024, 16), True, False)
            mm(x, r("nI"), r("Q", 256 * s + 64 * p, 256 * s + 64 * p + 64), False, True)

    def e_abs(p, h):
        act(r("Ea%d" % (p % 2), 512 * h, 512 * h + 512), r("p%d" % h), AF.Abs)

    def e_sum(p):
        for k in range(16):
            mm(r("p2", 64 * p, 64 * p + 64), r("WK", 128 * k, 128 * k + 128),
               r("Ea%d" % (p % 2), 64 * k, 64 * k + 64), k == 0, k == 15)

    nbuf = [0]

    def d_chunk(lst, bank, c):
        df, ab = "df%d" % (nbuf[0] % 3), "ab%d" % (nbuf[0] % 2)
        nbuf[0] += 1
        tt(r(df), ("ind", r("X"), r(lst, 64 * c, 64 * c + 64)), r("qrep", 1024 * c, 1024 * c + 1024), OP.subtract)
        act(r(ab), r(df), AF.Abs)
        for k in range(16):
            mm(r(bank, 64 * c, 64 * c + 64), r("WK", 128 * k, 128 * k + 128), r(ab, k, 1024, 16), k == 0, k == 15)

    def work(plan, s, gathers=()):
        for x in plan.split():
            k = int(x[1:] or 0)
            if x[0] == "G":
                e_gather(s, k)
            elif x[0] in "MN":
                e_minus(s, k, int(x[0] == "N"))
            elif x[0] in "AB":
                e_abs(k, int(x[0] == "B"))
            elif x[0] == "S":
                e_sum(k)
            elif x[0] == "C":
                act(r("E", 256 * s, 256 * s + 256), r("p2", 0, 256))
            elif x[0] == "D":
                d_chunk("pl", "p4" if k == 3 else "p3", k)
            elif x[0] == "V":
                d_chunk("PLE%d" % s, "p2", k)
            elif x[0] == "P":
                act(r("penal"), r("p5", 0, 256), AF.Abs, scale=8192.0)
            elif x[0] == "O":
                own(k)
            elif x[0] == "L":
                own_list(k)
            elif x[0] == "Q":
                act(r(gathers[k][0]), gathers[k][1])
                if k == 0:
                    for j in range(VREP + SREP, 16):
                        gcopy(r("qrep", j, 4096, 16), r("q"))
            elif x[0] == "R":
                act(r("qrep", VREP + k, 4096, 16), r("q"))

    own(0)
    for t in range(STEPS):
        last = t == STEPS - 1
        va, vb = "vT%d" % (t % 2), "vT%d" % ((t + 1) % 2)
        ca, cb = "vc%d" % (t % 2), "vc%d" % ((t + 1) % 2)
        ra, rb = "arep%d" % (t % 2), "arep%d" % ((t + 1) % 2)
        rw, aw = r("R", 0, COLS), r("A", 0, COLS)
        aT = r("sc", 15, 256, 16)
        if t > 0:
            tc(r("R", 6 + t - 1, COLS, 32), r("land", 128 * t - 128, 128 * t))
        act(r("e"), ("ind", rw, r("aL")))
        u = r("u") if t else r("U", 0, 256)
        two = ((0, 128), (128, 256))
        for a, b in two:
            tt(r("t1", a, b), ("ind", rw, r("aL", a // 16, b // 16)), (u[0], a, b, 1), OP.mult)
        for a, b in two:
            ts(r("t2", a, b), r("t1", a, b), 5, 4095, OP.arith_shift_right, OP.bitwise_and)
        for a, b in two:
            tt(r("t3", a, b), r("t2", a, b), r("e", a, b), OP.add)
        for a, b in two:
            ts(r("pl", a, b), r("t3", a, b), r("ckf"), None, OP.add)
        mm(r("p5", 0, 256), r("IBf"), r("e"))
        if t and t + 2 < STEPS:
            own(t + 2)
        if t == 0:
            own_list(0)
        work(FIRST if t == 0 else EARLY, t)
        if t + 2 < STEPS:
            own_list(t + 2)
        if t:
            tt(r("Ep"), ("ind", r("E", 0, 256 * t + 256), r("vcL")), r("penal"), OP.add)
            tt(r("oe"), ("ind", r("O", 0, 256 * t + 256), r("vcL")), r("e"), OP.subtract)
        else:
            tt(r("Ep"), r("E", 0, 256), r("penal"), OP.add)
            tt(r("oe"), r("O", 0, 256), r("e"), OP.subtract)
        if not last:
            work(TAIL, t + 1)
        halves = ((0, 192, "p3"), (192, LANES, "p4"))
        for a, b, bank in halves:
            tt(r("mn", a, b), r("Ep", a, b), r(bank, a, b), OP.min)
            ts(r("sf", a, b), r("mn", a, b), r("thb"), None, OP.is_lt)
        for k in range(16):
            mm(r("p6", 0, 16), r("WK", 128 * k, 128 * k + 128), r("sf", k, 256, 16), k == 0, k == 15)
        ts(r("Es"), r("Ep"), r("k0n"), None, OP.add)
        for a, b, bank in halves:
            tt(r("p7", 256 + a, 256 + b), r("Es", a, b), r(bank, a, b), OP.is_lt)
        tt(r("prod"), r("p7", 256, 512), r("oe"), OP.mult)
        ts(r("fT"), r("p6", 0, 16), 6.5, None, OP.is_ge)
        scan(r("incl"), r("ones", 0, 16), r("fT"), OP.mult, OP.add)
        mm(r("p5", 0, 16), r("U2"), r("fT"), True, False)
        mm(r("p5", 0, 16), r("BM"), r("incl"), False, True)
        ts(r("f256"), r("p6", 0, 16), 6.5, 256.0, OP.is_ge, OP.mult)
        ts(r("nf"), r("p6", 0, 16), 6.5, 4096.0, OP.is_lt, OP.mult)
        if not last:
            mm(r("p6", 64, 65), r("ones"), r("incl", 15, 16))
        tt(r("y"), r("p5", 0, 16), r("D0m"), OP.min)
        ts(r("offm"), r("y"), 1023.0, None, OP.add)
        tt(("ind", r("msg%d" % t), r("offm")), r("e"), r("prod"), OP.add)
        send(to(t), r("land", 128 * t, 128 * t + 128), r("msg%d" % t, 0, 128), "arr%d" % t)
        tt(r(cb), r(ca), r("f256"), OP.add)
        tt(r(vb), r(va), r("fT"), OP.add)
        tc(r("vcL"), r(cb))
        tt(r("dd"), r(vb), aT, OP.subtract)
        tt(r("y1"), r("dd"), r("fT"), OP.mult)
        tt(r("y3"), r("nf"), r(va), OP.add)
        tt(r("y2"), r("y1"), aT, OP.add)
        tc(r("offR"), r("y3"))
        tc(r("selL"), r("y2"))
        if not last:
            work(LATE, t + 1, [("q", ("ind", r("Q"), r("vcL"))), ("u", ("ind", r("U"), r("vcL"))), (rb, ("ind", aw, r("selL")))])
            tt(r("am"), ("ind", aw, r("selL")), r("diag"), OP.mult)
        else:
            act(r("vrep"), ("ind", r("VT"), r("vcL")))
            act(r(rb), ("ind", aw, r("selL")))
        tt(("ind", r("R"), r("offR")), r("e"), r("prod"), OP.add)
        if not last:
            scan(r("sc"), r("rz"), r("am"), OP.mult, OP.add)
            tc(r("bi"), r("p6", 64, 65))
            for k in range(VREP):
                tc(r("qrep", k, 4096, 16), r("q"))
                if k == 1:
                    tc(r("aL"), aT)
                if k == 3:
                    ts(r("bj"), r("bi"), 255, None, OP.bitwise_and)
                if k == 5:
                    tt(r("thb"), r("thf"), r("bj"), OP.add)
        if last:
            for s in range(3):
                act(r("p%d" % s, 0, 256), r("R", 3 + s, COLS, 16), AF.Copy, scale=4096.0)
                tt(r("yrt", s, 768, 3), r("p%d" % s, 0, 256), r("R", s, COLS, 16), OP.add)
        tc(("ind", r("A"), r("offR")), r(ra))
        if t > 0:
            gcopy(r("yht", t - 1, 768, 6), r("R", 6 + t - 1, COLS, 32))

    store(T.yv[:], T.l3[0:128:16, :], r("vrep"))
    store(T.ya[:], T["arep%d" % (STEPS % 2)][0:128:16, :], r("arep%d" % (STEPS % 2)))
    store(T.yr[:], T.U[:, 0:768], r("yrt", 0, 768))
    tc(r("yht", STEPS - 1, 768, 6), r("land", 128 * STEPS - 128, 128 * STEPS))
    store(T.yh[:], T.yht[:], r("yht"))
    for s in range(6):
        if s != 5:
            act(r("yant", s, 1536, 6), r("A", s, COLS, 16))
        else:
            tc(r("yant", s, 1536, 6), r("A", s, COLS, 16))
    store(T.yan[:], T.E[0:128:16, :], r("yant"))
    for sem in ("cv", "cs", "ct", "cg"):
        wait("g", sem, count[sem])
    g.wait_ge(T.sem["ls"], sent[0])
    g.wait_ge(T.sem["out"], stores[0])
